import numpy as np
import ml_dtypes


def mxq(x, axis, fmt="e4m3"):
    dtype, down = {"e4m3": (ml_dtypes.float8_e4m3fn, 7), "e5m2": (ml_dtypes.float8_e5m2, 14)}[fmt]
    v = np.moveaxis(np.asarray(x, np.float32).astype(ml_dtypes.bfloat16).astype(np.float64), axis, -1)
    blocks = v.reshape(v.shape[:-1] + (-1, 32))
    amax = np.abs(blocks).max(-1, keepdims=True)
    byte = np.maximum(np.where(amax > 0, np.frexp(amax)[1] - 1 + 127, 0) - down, 1)
    scale = np.exp2(byte - 127.0)
    codes = (blocks / scale).astype(np.float32).astype(dtype).astype(np.float64)
    return np.moveaxis((codes * scale).reshape(v.shape), -1, axis)


WIDE = False


def mx_kscale(k):
    if not WIDE:
        return np.ones(k)
    levels = np.array([30, -30])
    if k % 512:
        return np.exp2(np.random.permutation(np.resize(levels, k // 32))).repeat(32)
    a = np.empty((k // 512, 16))
    for p in range(k // 512):
        a[p, :8] = np.random.permutation(np.resize(levels, 8))
        for g in range(8):
            far = levels[np.abs(levels - a[p, g]) >= 10]
            a[p, g + 8] = far[np.random.randint(len(far))]
    return np.exp2(a.ravel()).repeat(32)


def f64(x):
    return np.asarray(x).astype(np.float64)


def striped(idx):
    return np.tile(np.asarray(idx).reshape(-1, 16).T, (8, 1)).astype(np.uint16)


def unstriped(offs):
    return offs[:16].T.reshape(-1).astype(np.int64)


E2M1 = np.array([0.0, 0.5, 1.0, 1.5, 2.0, 3.0, 4.0, 6.0, -0.0, -0.5, -1.0, -1.5, -2.0, -3.0, -4.0, -6.0])


def pack_weight(w, fmt):
    k, n = w.shape
    w = f64(np.asarray(w, np.float32).astype(ml_dtypes.bfloat16)).reshape(k // 32, 32, n)
    amax = np.abs(w).max(1)
    if fmt in ("e4m3", "e5m2"):
        byte = np.frexp(amax)[1] - 1 + 127 - (7 if fmt == "e4m3" else 14)
    else:
        mant, ex = np.frexp(amax / 6.0)
        byte = np.where(mant > 0.5, ex, ex - 1) + 127
    byte = np.clip(np.where(amax > 0, byte, 1), 1, 254)
    scaled = (w * np.exp2(127.0 - byte)[:, None, :]).reshape(k, n).astype(np.float32)
    by_word = np.ascontiguousarray(scaled.reshape(k // 512, 128, 4, n).transpose(0, 1, 3, 2))
    if fmt in ("e4m3", "e5m2"):
        words = by_word.astype(ml_dtypes.float8_e4m3fn if fmt == "e4m3" else ml_dtypes.float8_e5m2).view(np.uint8)
    else:
        c = by_word.astype(ml_dtypes.float4_e2m1fn).view(np.uint8) & 0xF
        words = (c[..., 0::2] | (c[..., 1::2] << 4)).reshape(k // 512, 128, 2 * n)
    return np.ascontiguousarray(words), np.ascontiguousarray(byte.astype(np.uint8).reshape(k // 512, 16, n))


def unpack_weight(words, scales, fmt):
    g, _, n = scales.shape
    words = np.ascontiguousarray(words).reshape(g, 128, n, -1)
    if fmt in ("e4m3", "e5m2"):
        vals = words.view(ml_dtypes.float8_e4m3fn if fmt == "e4m3" else ml_dtypes.float8_e5m2).astype(np.float64)
    else:
        nib = np.empty((g, 128, n, 4), np.uint8)
        nib[..., 0::2] = words & 0xF
        nib[..., 1::2] = words >> 4
        vals = E2M1[nib]
    vals = vals * np.repeat(np.exp2(scales.astype(np.float64) - 127.0), 8, axis=1)[..., None]
    return vals.transpose(0, 1, 3, 2).reshape(g * 512, n)


K, T, J, R, C, O, N, E = 512, 1024, 256, 512, 512, 256, 256, 128


def setup_inputs():
    n = np.random.standard_normal
    idx = np.random.permutation(T)[:J]
    idx2 = np.random.permutation(C)[:J]
    idx3 = np.random.permutation(C)[:C]
    idx4 = np.random.permutation(C)[:O]
    idx5 = np.random.permutation(T)[:O]
    idx6 = np.random.permutation(O)[:E]
    idx7 = np.random.permutation(O)[:E]
    fk = mx_kscale(K)
    fr = mx_kscale(R)
    xtp = pack_weight(n((K, T)) / fk[:, None], "e4m3")
    wp = pack_weight(n((K, R)) * 1 / np.sqrt(K) * fk[:, None] * fr, "e2m1")
    wbp = pack_weight(n((R, N)) * 1 / np.sqrt(R) / fr[:, None], "e5m2")
    wsp = pack_weight(n((K, N)) * 1 / np.sqrt(K) * fk[:, None], "e5m2")
    return {
        "xt_words": xtp[0],
        "xt_scales": xtp[1],
        "w_words": wp[0],
        "w_scales": wp[1],
        "wb_words": wbp[0],
        "wb_scales": wbp[1],
        "ws_words": wsp[0],
        "ws_scales": wsp[1],
        "offs": striped(idx),
        "offs2": striped(idx2),
        "offs3": striped(idx3),
        "offs4": striped(idx4),
        "offs5": striped(idx5),
        "offs6": striped(idx6),
        "offs7": striped(idx7),
    }


def reference(xt_words, xt_scales, w_words, w_scales, wb_words, wb_scales, ws_words, ws_scales, offs, offs2, offs3, offs4, offs5, offs6, offs7):
    idx = unstriped(offs)
    idx2 = unstriped(offs2)
    idx3 = unstriped(offs3)
    idx4 = unstriped(offs4)
    idx5 = unstriped(offs5)
    idx6 = unstriped(offs6)
    idx7 = unstriped(offs7)
    xtu = unpack_weight(xt_words, xt_scales, "e4m3")
    wu = unpack_weight(w_words, w_scales, "e2m1")
    wbu = unpack_weight(wb_words, wb_scales, "e5m2")
    wsu = unpack_weight(ws_words, ws_scales, "e5m2")
    xtidxg = xtu[:, idx]
    a = wu.T @ xtidxg
    pw = np.zeros((R, C))
    pw[:, idx2] = a
    pg = np.maximum(pw, pw[:, idx3])
    hid = pg[:, idx4]
    hidq = mxq(hid, 0, "e4m3")
    xtidx5g = xtu[:, idx5]
    p = wbu.T @ hidq + wsu.T @ xtidx5g
    y = np.maximum(p[:, idx6], p[:, idx7])
    return y

@@ -1,0 +1,153 @@
+from contextlib import ExitStack
+
+import concourse.mybir as mybir
+
+K, T, J, R, C, O, N, E = 512, 1024, 256, 512, 512, 256, 256, 128
+FLOPS = 2 * K * R * J + 2 * R * N * O + 2 * K * N * O
+
+F32 = mybir.dt.float32
+BF16 = mybir.dt.bfloat16
+I32 = mybir.dt.int32
+U32 = mybir.dt.uint32
+U16 = mybir.dt.uint16
+U8 = mybir.dt.uint8
+E4M3 = mybir.dt.float8_e4m3fn_x4
+E5M2 = mybir.dt.float8_e5m2_x4
+E2M1 = mybir.dt.float4_e2m1fn_x4
+COPY = mybir.ActivationFunctionType.Copy
+MAX = mybir.AluOpType.max
+
+P = 128
+PACK = 4
+
+
+def tile_list_boardladder_solo_further_bestoftwo_kernel(
+    tc, xt_words, xt_scales, w_words, w_scales, wb_words, wb_scales, ws_words, ws_scales,
+    offs, offs2, offs3, offs4, offs5, offs6, offs7, out,
+):
+    nc = tc.nc
+    with ExitStack() as ctx:
+        keep = ctx.enter_context(tc.tile_pool(name="keep", bufs=1))
+        psum = ctx.enter_context(tc.psum_pool(name="psum", bufs=1))
+
+        def load_list(src, name):
+            dst = keep.tile(list(src.shape), U16, name=name)
+            nc.sync.dma_start(dst[:], src)
+            return dst
+
+        def load_words(queue, src, dtype, columns, name):
+            dst = keep.tile([P, columns], dtype, name=name, align_bytes=64)
+            queue.dma_start(dst[:].bitcast(I32), src.bitcast(I32))
+            return dst
+
+        def load_scales(queues, src, name):
+            columns = src.shape[2]
+            dst = keep.tile([P, columns], U8, name=name, align_bytes=64)
+            nc.vector.memset(dst[:].bitcast(I32), 0)
+            return dst, [
+                (queues[q], dst[32 * q : 32 * q + 4, :].bitcast(I32), src[0, 4 * q : 4 * q + 4, :].bitcast(I32))
+                for q in range(4)
+            ]
+
+        def start(loads):
+            for queue, dst, src in loads:
+                queue.dma_start(dst, src)
+
+        def move(engine, dst, src):
+            if engine is nc.scalar:
+                nc.scalar.activation(dst, src, COPY)
+            else:
+                nc.vector.tensor_copy(dst, src)
+
+        xs, xs_loads = load_scales([nc.scalar, nc.scalar, nc.sync, nc.sync], xt_scales, "xs")
+        wsc, wsc_loads = load_scales([nc.scalar, nc.sync, nc.sync, nc.sync], w_scales, "wsc")
+        ss, ss_loads = load_scales([nc.sync] * 4, ws_scales, "ss")
+        bs, bs_loads = load_scales([nc.sync] * 4, wb_scales, "bs")
+        l1 = load_list(offs, "l1")
+        ww = load_words(nc.sync, w_words[0], U16, R, "ww")
+        start(xs_loads)
+        xw = load_words(nc.sync, xt_words[0].rearrange("p n t -> p (n t)"), U32, T, "xw")
+        start(wsc_loads)
+        l5 = load_list(offs5, "l5")
+        l2 = load_list(offs2, "l2")
+        l3 = load_list(offs3, "l3")
+        l4 = load_list(offs4, "l4")
+        sw = load_words(nc.sync, ws_words[0].rearrange("p n t -> p (n t)"), U32, N, "sw")
+        start(ss_loads)
+        bw = load_words(nc.sync, wb_words[0].rearrange("p n t -> p (n t)"), U32, N, "bw")
+        start(bs_loads)
+        l6 = load_list(offs6, "l6")
+        l7 = load_list(offs7, "l7")
+
+        pw = [keep.tile([P, C], F32, name="pw%d" % t) for t in range(PACK)]
+        for t in range(PACK):
+            nc.vector.memset(pw[t][:], 0.0)
+
+        x1s = keep.tile([P, J], U8, align_bytes=64)
+        nc.vector.tensor_copy(x1s[:], xs[:].indirect(l1[:]))
+        wd = keep.tile([P, R], U16, align_bytes=64)
+        nc.vector.tensor_copy(wd[:].rearrange("p (t q) -> p t q", t=PACK), ww[:].rearrange("p (q t) -> p t q", t=PACK))
+        x1w = keep.tile([P, J], U32, align_bytes=64)
+        nc.vector.tensor_copy(x1w[:], xw[:].indirect(l1[:]))
+        wds = [keep.tile([P, P], U8, name="wds%d" % t, align_bytes=64) for t in range(PACK)]
+        for t in range(PACK):
+            nc.vector.tensor_copy(wds[t][:], wsc[:, t::PACK])
+
+        a = []
+        for t in range(PACK):
+            bank = psum.tile([P, J], F32, name="a_bank%d" % t)
+            cols = slice(P * t, P * (t + 1))
+            nc.tensor.matmul_mx(out=bank[:], lhsT=wd[:, cols].bitcast(E2M1), lhsT_scale=wds[t][:],
+                                rhs=x1w[:].bitcast(E4M3), rhs_scale=x1s[:], start=True, stop=True)
+            a.append(keep.tile([P, J], F32, name="a%d" % t))
+            nc.scalar.copy(a[t][:], bank[:])
+
+        x5s = keep.tile([P, O], U8, align_bytes=64)
+        nc.vector.tensor_copy(x5s[:], xs[:].indirect(l5[:]))
+        x5w = keep.tile([P, O], U32, align_bytes=64)
+        nc.vector.tensor_copy(x5w[:], xw[:].indirect(l5[:]))
+        p_bank = [psum.tile([P, O], F32, name="p_bank%d" % h) for h in range(2)]
+        for h in range(2):
+            cols = slice(P * h, P * (h + 1))
+            nc.tensor.matmul_mx(out=p_bank[h][:], lhsT=sw[:, cols].bitcast(E5M2), lhsT_scale=ss[:, cols],
+                                rhs=x5w[:].bitcast(E4M3), rhs_scale=x5s[:], start=True, stop=False)
+
+        owner = [nc.vector, nc.scalar, nc.vector, nc.scalar]
+        for t in range(PACK):
+            move(owner[t], pw[t][:].indirect(l2[:]), a[t][:])
+        other = [keep.tile([P, C], F32, name="other%d" % t) for t in range(PACK)]
+        pg = [keep.tile([P, C], F32, name="pg%d" % t) for t in range(PACK)]
+        for t in range(PACK):
+            for u in range(2):
+                move(owner[t], other[t][:, 256 * u : 256 * (u + 1)], pw[t][:].indirect(l3[:, 16 * u : 16 * (u + 1)]))
+        hid = keep.tile([P, PACK, O], BF16)
+        for t in range(PACK):
+            nc.vector.tensor_tensor(pg[t][:], pw[t][:], other[t][:], MAX)
+            if t < PACK - 1:
+                move(nc.scalar, hid[:, t, :], pg[t][:].indirect(l4[:]))
+            else:
+                move(nc.vector, hid[:, t, :128], pg[t][:].indirect(l4[:, :8]))
+                move(nc.scalar, hid[:, t, 128:], pg[t][:].indirect(l4[:, 8:]))
+        woven = [keep.tile([P, 128, PACK], BF16, name="woven%d" % u, align_bytes=64) for u in range(2)]
+        hw = [keep.tile([P, 128], U32, name="hw%d" % u, align_bytes=64) for u in range(2)]
+        hs = [keep.tile([P, 128], U8, name="hs%d" % u, align_bytes=64) for u in range(2)]
+        for u in range(2):
+            nc.vector.tensor_copy(woven[u][:], hid[:, :, 128 * u : 128 * (u + 1)].rearrange("p t o -> p o t"))
+        for u in range(2):
+            nc.vector.quantize_mx(out=hw[u][:].bitcast(E4M3), scales=hs[u][:], in_=woven[u][:].rearrange("p o t -> p (o t)"))
+        for u in range(2):
+            for h in range(2):
+                cols = slice(P * h, P * (h + 1))
+                nc.tensor.matmul_mx(out=p_bank[h][:, 128 * u : 128 * (u + 1)], lhsT=bw[:, cols].bitcast(E5M2), lhsT_scale=bs[:, cols],
+                                    rhs=hw[u][:].bitcast(E4M3), rhs_scale=hs[u][:], start=False, stop=(u == 1))
+        for h in range(2):
+            engine = (nc.vector, nc.scalar)[h]
+            p_sb = keep.tile([P, O], F32, name="p%d" % h)
+            move(engine, p_sb[:], p_bank[h][:])
+            first = keep.tile([P, E], F32, name="first%d" % h)
+            second = keep.tile([P, E], F32, name="second%d" % h)
+            move(engine, first[:], p_sb[:].indirect(l6[:]))
+            move(engine, second[:], p_sb[:].indirect(l7[:]))
+            best = keep.tile([P, E], F32, name="best%d" % h)
+            nc.vector.tensor_tensor(best[:], first[:], second[:], MAX)
+            nc.sync.dma_start(out[P * h : P * (h + 1), :], best[:])

@@ -60,15 +60,15 @@ def tile_list_boardladder_solo_further_bestoftwo_kernel(
                 nc.vector.tensor_copy(dst, src)
 
         xs, xs_loads = load_scales([nc.scalar, nc.scalar, nc.sync, nc.sync], xt_scales, "xs")
-        wsc, wsc_loads = load_scales([nc.scalar, nc.sync, nc.sync, nc.sync], w_scales, "wsc")
+        wsc, wsc_loads = load_scales([nc.sync] * 4, w_scales, "wsc")
         ss, ss_loads = load_scales([nc.sync] * 4, ws_scales, "ss")
         bs, bs_loads = load_scales([nc.sync] * 4, wb_scales, "bs")
         l1 = load_list(offs, "l1")
         ww = load_words(nc.sync, w_words[0], U16, R, "ww")
+        l5 = load_list(offs5, "l5")
         start(xs_loads)
         xw = load_words(nc.sync, xt_words[0].rearrange("p n t -> p (n t)"), U32, T, "xw")
         start(wsc_loads)
-        l5 = load_list(offs5, "l5")
         l2 = load_list(offs2, "l2")
         l3 = load_list(offs3, "l3")
         l4 = load_list(offs4, "l4")
@@ -87,6 +87,8 @@ def tile_list_boardladder_solo_further_bestoftwo_kernel(
         nc.vector.tensor_copy(x1s[:], xs[:].indirect(l1[:]))
         wd = keep.tile([P, R], U16, align_bytes=64)
         nc.vector.tensor_copy(wd[:].rearrange("p (t q) -> p t q", t=PACK), ww[:].rearrange("p (q t) -> p t q", t=PACK))
+        x5s = keep.tile([P, O], U8, align_bytes=64)
+        nc.vector.tensor_copy(x5s[:], xs[:].indirect(l5[:]))
         x1w = keep.tile([P, J], U32, align_bytes=64)
         nc.vector.tensor_copy(x1w[:], xw[:].indirect(l1[:]))
         wds = [keep.tile([P, P], U8, name="wds%d" % t, align_bytes=64) for t in range(PACK)]
@@ -102,17 +104,17 @@ def tile_list_boardladder_solo_further_bestoftwo_kernel(
             a.append(keep.tile([P, J], F32, name="a%d" % t))
             nc.scalar.copy(a[t][:], bank[:])
 
-        x5s = keep.tile([P, O], U8, align_bytes=64)
-        nc.vector.tensor_copy(x5s[:], xs[:].indirect(l5[:]))
-        x5w = keep.tile([P, O], U32, align_bytes=64)
+        x5w = keep.tile([P, O], U32, align_bytes=64, tag="wsc")
         nc.vector.tensor_copy(x5w[:], xw[:].indirect(l5[:]))
-        p_bank = [psum.tile([P, O], F32, name="p_bank%d" % h) for h in range(2)]
-        for h in range(2):
-            cols = slice(P * h, P * (h + 1))
-            nc.tensor.matmul_mx(out=p_bank[h][:], lhsT=sw[:, cols].bitcast(E5M2), lhsT_scale=ss[:, cols],
-                                rhs=x5w[:].bitcast(E4M3), rhs_scale=x5s[:], start=True, stop=False)
+        p_bank = [[psum.tile([P, 128], F32, name="p_bank%d%d" % (h, u)) for u in range(2)] for h in range(2)]
+        for u in range(2):
+            for h in range(2):
+                cols = slice(P * h, P * (h + 1))
+                reads = slice(128 * u, 128 * (u + 1))
+                nc.tensor.matmul_mx(out=p_bank[h][u][:], lhsT=sw[:, cols].bitcast(E5M2), lhsT_scale=ss[:, cols],
+                                    rhs=x5w[:, reads].bitcast(E4M3), rhs_scale=x5s[:, reads], start=True, stop=False)
 
-        owner = [nc.vector, nc.scalar, nc.vector, nc.scalar]
+        owner = [nc.vector, nc.vector, nc.scalar, nc.scalar]
         for t in range(PACK):
             move(owner[t], pw[t][:].indirect(l2[:]), a[t][:])
         other = [keep.tile([P, C], F32, name="other%d" % t) for t in range(PACK)]
@@ -120,34 +122,36 @@ def tile_list_boardladder_solo_further_bestoftwo_kernel(
         for t in range(PACK):
             for u in range(2):
                 move(owner[t], other[t][:, 256 * u : 256 * (u + 1)], pw[t][:].indirect(l3[:, 16 * u : 16 * (u + 1)]))
-        hid = keep.tile([P, PACK, O], BF16)
         for t in range(PACK):
             nc.vector.tensor_tensor(pg[t][:], pw[t][:], other[t][:], MAX)
-            if t < PACK - 1:
-                move(nc.scalar, hid[:, t, :], pg[t][:].indirect(l4[:]))
-            else:
-                move(nc.vector, hid[:, t, :128], pg[t][:].indirect(l4[:, :8]))
-                move(nc.scalar, hid[:, t, 128:], pg[t][:].indirect(l4[:, 8:]))
+        hid = keep.tile([P, PACK, O], BF16)
+        for t in (0, 1):
+            move(nc.scalar, hid[:, t, :], pg[t][:].indirect(l4[:]))
+        for t in (2, 3):
+            for u in range(2):
+                engine = nc.vector if t + u == 3 else nc.scalar
+                move(engine, hid[:, t, 128 * u : 128 * (u + 1)], pg[t][:].indirect(l4[:, 8 * u : 8 * (u + 1)]))
         woven = [keep.tile([P, 128, PACK], BF16, name="woven%d" % u, align_bytes=64) for u in range(2)]
         hw = [keep.tile([P, 128], U32, name="hw%d" % u, align_bytes=64) for u in range(2)]
         hs = [keep.tile([P, 128], U8, name="hs%d" % u, align_bytes=64) for u in range(2)]
-        for u in range(2):
-            nc.vector.tensor_copy(woven[u][:], hid[:, :, 128 * u : 128 * (u + 1)].rearrange("p t o -> p o t"))
-        for u in range(2):
+        nc.vector.tensor_copy(woven[1][:], hid[:, :, 128:].rearrange("p t o -> p o t"))
+        nc.scalar.copy(woven[0][:], hid[:, :, :128].rearrange("p t o -> p o t"))
+        for u in (1, 0):
             nc.vector.quantize_mx(out=hw[u][:].bitcast(E4M3), scales=hs[u][:], in_=woven[u][:].rearrange("p o t -> p (o t)"))
-        for u in range(2):
+        p_sb = [keep.tile([P, O], F32, name="p%d" % h) for h in range(2)]
+        for u in (1, 0):
             for h in range(2):
                 cols = slice(P * h, P * (h + 1))
-                nc.tensor.matmul_mx(out=p_bank[h][:, 128 * u : 128 * (u + 1)], lhsT=bw[:, cols].bitcast(E5M2), lhsT_scale=bs[:, cols],
-                                    rhs=hw[u][:].bitcast(E4M3), rhs_scale=hs[u][:], start=False, stop=(u == 1))
+                nc.tensor.matmul_mx(out=p_bank[h][u][:], lhsT=bw[:, cols].bitcast(E5M2), lhsT_scale=bs[:, cols],
+                                    rhs=hw[u][:].bitcast(E4M3), rhs_scale=hs[u][:], start=False, stop=True)
+                engine = nc.vector if (h, u) == (0, 0) else nc.scalar
+                move(engine, p_sb[h][:, 128 * u : 128 * (u + 1)], p_bank[h][u][:])
+        first = [keep.tile([P, E], F32, name="first%d" % h) for h in range(2)]
+        second = [keep.tile([P, E], F32, name="second%d" % h) for h in range(2)]
         for h in range(2):
-            engine = (nc.vector, nc.scalar)[h]
-            p_sb = keep.tile([P, O], F32, name="p%d" % h)
-            move(engine, p_sb[:], p_bank[h][:])
-            first = keep.tile([P, E], F32, name="first%d" % h)
-            second = keep.tile([P, E], F32, name="second%d" % h)
-            move(engine, first[:], p_sb[:].indirect(l6[:]))
-            move(engine, second[:], p_sb[:].indirect(l7[:]))
+            move(nc.vector, first[h][:], p_sb[h][:].indirect(l6[:]))
+            move(nc.scalar, second[h][:], p_sb[h][:].indirect(l7[:]))
+        for h in range(2):
             best = keep.tile([P, E], F32, name="best%d" % h)
-            nc.vector.tensor_tensor(best[:], first[:], second[:], MAX)
+            nc.vector.tensor_tensor(best[:], first[h][:], second[h][:], MAX)
             nc.sync.dma_start(out[P * h : P * (h + 1), :], best[:])

from contextlib import ExitStack

import concourse.mybir as mybir

K, T, J, R, C, O, N, E = 512, 1024, 256, 512, 512, 256, 256, 128
FLOPS = 2 * K * R * J + 2 * R * N * O + 2 * K * N * O

F32 = mybir.dt.float32
BF16 = mybir.dt.bfloat16
I32 = mybir.dt.int32
U32 = mybir.dt.uint32
U16 = mybir.dt.uint16
U8 = mybir.dt.uint8
E4M3 = mybir.dt.float8_e4m3fn_x4
E5M2 = mybir.dt.float8_e5m2_x4
E2M1 = mybir.dt.float4_e2m1fn_x4
COPY = mybir.ActivationFunctionType.Copy
MAX = mybir.AluOpType.max

P = 128
PACK = 4


def tile_list_boardladder_solo_further_bestoftwo_kernel(
    tc, xt_words, xt_scales, w_words, w_scales, wb_words, wb_scales, ws_words, ws_scales,
    offs, offs2, offs3, offs4, offs5, offs6, offs7, out,
):
    nc = tc.nc
    with ExitStack() as ctx:
        keep = ctx.enter_context(tc.tile_pool(name="keep", bufs=1))
        psum = ctx.enter_context(tc.psum_pool(name="psum", bufs=1))

        def load_list(src, name):
            dst = keep.tile(list(src.shape), U16, name=name)
            nc.sync.dma_start(dst[:], src)
            return dst

        def load_words(queue, src, dtype, columns, name):
            dst = keep.tile([P, columns], dtype, name=name, align_bytes=64)
            queue.dma_start(dst[:].bitcast(I32), src.bitcast(I32))
            return dst

        def load_scales(queues, src, name):
            columns = src.shape[2]
            dst = keep.tile([P, columns], U8, name=name, align_bytes=64)
            nc.vector.memset(dst[:].bitcast(I32), 0)
            return dst, [
                (queues[q], dst[32 * q : 32 * q + 4, :].bitcast(I32), src[0, 4 * q : 4 * q + 4, :].bitcast(I32))
                for q in range(4)
            ]

        def start(loads):
            for queue, dst, src in loads:
                queue.dma_start(dst, src)

        def move(engine, dst, src):
            if engine is nc.scalar:
                nc.scalar.activation(dst, src, COPY)
            else:
                nc.vector.tensor_copy(dst, src)

        xs, xs_loads = load_scales([nc.scalar, nc.scalar, nc.sync, nc.sync], xt_scales, "xs")
        wsc, wsc_loads = load_scales([nc.sync] * 4, w_scales, "wsc")
        ss, ss_loads = load_scales([nc.sync] * 4, ws_scales, "ss")
        bs, bs_loads = load_scales([nc.sync] * 4, wb_scales, "bs")
        l1 = load_list(offs, "l1")
        ww = load_words(nc.sync, w_words[0], U16, R, "ww")
        l5 = load_list(offs5, "l5")
        start(xs_loads)
        xw = load_words(nc.sync, xt_words[0].rearrange("p n t -> p (n t)"), U32, T, "xw")
        start(wsc_loads)
        l2 = load_list(offs2, "l2")
        l3 = load_list(offs3, "l3")
        l4 = load_list(offs4, "l4")
        sw = load_words(nc.sync, ws_words[0].rearrange("p n t -> p (n t)"), U32, N, "sw")
        start(ss_loads)
        bw = load_words(nc.sync, wb_words[0].rearrange("p n t -> p (n t)"), U32, N, "bw")
        start(bs_loads)
        l6 = load_list(offs6, "l6")
        l7 = load_list(offs7, "l7")

        pw = [keep.tile([P, C], F32, name="pw%d" % t) for t in range(PACK)]
        for t in range(PACK):
            nc.vector.memset(pw[t][:], 0.0)

        x1s = keep.tile([P, J], U8, align_bytes=64)
        nc.vector.tensor_copy(x1s[:], xs[:].indirect(l1[:]))
        wd = keep.tile([P, R], U16, align_bytes=64)
        nc.vector.tensor_copy(wd[:].rearrange("p (t q) -> p t q", t=PACK), ww[:].rearrange("p (q t) -> p t q", t=PACK))
        x5s = keep.tile([P, O], U8, align_bytes=64)
        nc.vector.tensor_copy(x5s[:], xs[:].indirect(l5[:]))
        x1w = keep.tile([P, J], U32, align_bytes=64)
        nc.vector.tensor_copy(x1w[:], xw[:].indirect(l1[:]))
        wds = [keep.tile([P, P], U8, name="wds%d" % t, align_bytes=64) for t in range(PACK)]
        for t in range(PACK):
            nc.vector.tensor_copy(wds[t][:], wsc[:, t::PACK])

        a = []
        for t in range(PACK):
            bank = psum.tile([P, J], F32, name="a_bank%d" % t)
            cols = slice(P * t, P * (t + 1))
            nc.tensor.matmul_mx(out=bank[:], lhsT=wd[:, cols].bitcast(E2M1), lhsT_scale=wds[t][:],
                                rhs=x1w[:].bitcast(E4M3), rhs_scale=x1s[:], start=True, stop=True)
            a.append(keep.tile([P, J], F32, name="a%d" % t))
            nc.scalar.copy(a[t][:], bank[:])

        x5w = keep.tile([P, O], U32, align_bytes=64, tag="wsc")
        nc.vector.tensor_copy(x5w[:], xw[:].indirect(l5[:]))
        p_bank = [[psum.tile([P, 128], F32, name="p_bank%d%d" % (h, u)) for u in range(2)] for h in range(2)]
        for u in range(2):
            for h in range(2):
                cols = slice(P * h, P * (h + 1))
                reads = slice(128 * u, 128 * (u + 1))
                nc.tensor.matmul_mx(out=p_bank[h][u][:], lhsT=sw[:, cols].bitcast(E5M2), lhsT_scale=ss[:, cols],
                                    rhs=x5w[:, reads].bitcast(E4M3), rhs_scale=x5s[:, reads], start=True, stop=False)

        owner = [nc.vector, nc.vector, nc.scalar, nc.scalar]
        for t in range(PACK):
            move(owner[t], pw[t][:].indirect(l2[:]), a[t][:])
        other = [keep.tile([P, C], F32, name="other%d" % t) for t in range(PACK)]
        pg = [keep.tile([P, C], F32, name="pg%d" % t) for t in range(PACK)]
        for t in range(PACK):
            for u in range(2):
                move(owner[t], other[t][:, 256 * u : 256 * (u + 1)], pw[t][:].indirect(l3[:, 16 * u : 16 * (u + 1)]))
        for t in range(PACK):
            nc.vector.tensor_tensor(pg[t][:], pw[t][:], other[t][:], MAX)
        hid = keep.tile([P, PACK, O], BF16)
        for t in (0, 1):
            move(nc.scalar, hid[:, t, :], pg[t][:].indirect(l4[:]))
        for t in (2, 3):
            for u in range(2):
                engine = nc.vector if t + u == 3 else nc.scalar
                move(engine, hid[:, t, 128 * u : 128 * (u + 1)], pg[t][:].indirect(l4[:, 8 * u : 8 * (u + 1)]))
        woven = [keep.tile([P, 128, PACK], BF16, name="woven%d" % u, align_bytes=64) for u in range(2)]
        hw = [keep.tile([P, 128], U32, name="hw%d" % u, align_bytes=64) for u in range(2)]
        hs = [keep.tile([P, 128], U8, name="hs%d" % u, align_bytes=64) for u in range(2)]
        nc.vector.tensor_copy(woven[1][:], hid[:, :, 128:].rearrange("p t o -> p o t"))
        nc.scalar.copy(woven[0][:], hid[:, :, :128].rearrange("p t o -> p o t"))
        for u in (1, 0):
            nc.vector.quantize_mx(out=hw[u][:].bitcast(E4M3), scales=hs[u][:], in_=woven[u][:].rearrange("p o t -> p (o t)"))
        p_sb = [keep.tile([P, O], F32, name="p%d" % h) for h in range(2)]
        for u in (1, 0):
            for h in range(2):
                cols = slice(P * h, P * (h + 1))
                nc.tensor.matmul_mx(out=p_bank[h][u][:], lhsT=bw[:, cols].bitcast(E5M2), lhsT_scale=bs[:, cols],
                                    rhs=hw[u][:].bitcast(E4M3), rhs_scale=hs[u][:], start=False, stop=True)
                engine = nc.vector if (h, u) == (0, 0) else nc.scalar
                move(engine, p_sb[h][:, 128 * u : 128 * (u + 1)], p_bank[h][u][:])
        first = [keep.tile([P, E], F32, name="first%d" % h) for h in range(2)]
        second = [keep.tile([P, E], F32, name="second%d" % h) for h in range(2)]
        for h in range(2):
            move(nc.vector, first[h][:], p_sb[h][:].indirect(l6[:]))
            move(nc.scalar, second[h][:], p_sb[h][:].indirect(l7[:]))
        for h in range(2):
            best = keep.tile([P, E], F32, name="best%d" % h)
            nc.vector.tensor_tensor(best[:], first[h][:], second[h][:], MAX)
            nc.sync.dma_start(out[P * h : P * (h + 1), :], best[:])
